import numpy as np
import ml_dtypes


def mxq(x, axis, fmt="e4m3"):
    dtype, down = {"e4m3": (ml_dtypes.float8_e4m3fn, 7), "e5m2": (ml_dtypes.float8_e5m2, 14)}[fmt]
    v = np.moveaxis(np.asarray(x, np.float32).astype(ml_dtypes.bfloat16).astype(np.float64), axis, -1)
    blocks = v.reshape(v.shape[:-1] + (-1, 32))
    amax = np.abs(blocks).max(-1, keepdims=True)
    byte = np.maximum(np.where(amax > 0, np.frexp(amax)[1] - 1 + 127, 0) - down, 1)
    scale = np.exp2(byte - 127.0)
    codes = (blocks / scale).astype(np.float32).astype(dtype).astype(np.float64)
    return np.moveaxis((codes * scale).reshape(v.shape), -1, axis)


WIDE = False


def mx_kscale(k):
    if not WIDE:
        return np.ones(k)
    levels = np.array([10, -10, 5, -5, 0])
    if k % 512:
        return np.exp2(np.random.permutation(np.resize(levels, k // 32))).repeat(32)
    a = np.empty((k // 512, 16))
    for p in range(k // 512):
        a[p, :8] = np.random.permutation(np.resize(levels, 8))
        for g in range(8):
            far = levels[np.abs(levels - a[p, g]) >= 10]
            a[p, g + 8] = far[np.random.randint(len(far))]
    return np.exp2(a.ravel()).repeat(32)


def f64(x):
    return np.asarray(x).astype(np.float64)


def striped(idx):
    return np.tile(idx.reshape(-1, 16).T, (8, 1)).astype(np.uint16)


def unstriped(offs):
    return offs[:16].T.reshape(-1).astype(np.int64)


def silu(v):
    return v / (1.0 + np.exp(-np.maximum(v, -700.0)))


K, T, E, C, H, N = 512, 768, 6, 256, 1024, 128


def by_expert(wq, xq):
    return np.concatenate([wq[e].T @ xq[:, e * C:(e + 1) * C] for e in range(E)], axis=1)


def setup_inputs():
    n = np.random.standard_normal
    s = mx_kscale(K)[:, None]
    u = mx_kscale(H)
    first = np.random.permutation(np.repeat(np.arange(E), T // E))
    second = (first + 1 + np.random.permutation(np.repeat(np.arange(E - 1), -(-T // (E - 1)))[:T])) % E
    while np.bincount(second, minlength=E).max() != T // E:
        load = np.bincount(second, minlength=E); hi, lo = int(load.argmax()), int(load.argmin())
        t = np.flatnonzero((second == hi) & (first != lo))[0]; second[t] = lo
    slot_token = np.empty(E * C, np.int64); pos = np.empty((2, T), np.int64); fill = np.zeros(E, np.int64)
    place = np.stack([np.random.permutation(C) for _ in range(E)])
    for r, deal in enumerate((first, second)):
        for t in np.random.permutation(T):
            e = deal[t]; j = e * C + place[e, fill[e]]; fill[e] += 1; slot_token[j] = t; pos[r, t] = j
    g = np.random.uniform(0.2, 0.8, T)
    return {
        "xT": (n((K, T)) * s).astype(np.float32),
        "w1": (n((E + 1, K, H)) / np.sqrt(K) / s[None] * u[None, None, :]).astype(np.float32),
        "w2": (n((E + 1, H, N)) / np.sqrt(H) / u[None, :, None]).astype(np.float32),
        "gate": np.stack([np.tile(g, (N, 1)), np.tile(1.0 - g, (N, 1))]).astype(np.float32),
        "offs": striped(slot_token),
        "pos1": striped(pos[0]),
        "pos2": striped(pos[1]),
    }


def reference(xT, w1, w2, gate, offs, pos1, pos2):
    idx = unstriped(offs)
    w1q, w2q = mxq(f64(w1), 1, "e4m3"), mxq(f64(w2), 1, "e4m3")
    xs = mxq(f64(xT), 0, "e4m3")
    hs = silu(w1q[E].T @ xs)
    ys = w2q[E].T @ mxq(hs, 0, "e4m3")
    xq = mxq(f64(xT)[:, idx], 0, "e4m3")
    h = silu(by_expert(w1q, xq))
    y = by_expert(w2q, mxq(h, 0, "e4m3"))
    return ys + f64(gate[0]) * y[:, unstriped(pos1)] + f64(gate[1]) * y[:, unstriped(pos2)]

@@ -1,0 +1,303 @@
+from contextlib import ExitStack
+
+import concourse.mybir as mybir
+
+K, T, E, C, H, N = 512, 768, 6, 256, 1024, 128
+FLOPS = 2 * (E * C + T) * (K * H + H * N)
+
+F32 = mybir.dt.float32
+BF16 = mybir.dt.bfloat16
+U32 = mybir.dt.uint32
+U16 = mybir.dt.uint16
+U8 = mybir.dt.uint8
+FP8X4 = mybir.dt.float8_e4m3fn_x4
+SILU = mybir.ActivationFunctionType.Silu
+ADD = mybir.AluOpType.add
+MULT = mybir.AluOpType.mult
+
+P = 128
+J = 4
+K_PASS = P * J
+HALVES = H // K_PASS
+SHARED = E
+SHARED_GROUPS = T // C
+SCALAR_W1 = [(0, 1)] + [(e, 0) for e in range(E + 1)]
+SCALAR_W2 = [0, 1, 2, 3, 6]
+J_PIECE = 2
+
+
+def tile_moe_shr_mlp_silu_kernel(tc, xT, w1, w2, gate, offs, pos1, pos2, out):
+    nc = tc.nc
+    with ExitStack() as ctx:
+        keep = ctx.enter_context(tc.tile_pool(name="keep", bufs=1))
+        raws = ctx.enter_context(tc.tile_pool(name="raws", bufs=8))
+        raws2 = ctx.enter_context(tc.tile_pool(name="raws2", bufs=7))
+        values = ctx.enter_context(tc.tile_pool(name="values", bufs=4))
+        single = ctx.enter_context(tc.tile_pool(name="single", bufs=2))
+        pair = ctx.enter_context(tc.tile_pool(name="pair", bufs=2))
+        codes = ctx.enter_context(tc.tile_pool(name="codes", bufs=4))
+        hidden = ctx.enter_context(tc.tile_pool(name="hidden", bufs=10))
+        psum_a = ctx.enter_context(tc.psum_pool(name="psum_a", bufs=5))
+        psum_y = ctx.enter_context(tc.psum_pool(name="psum_y", bufs=3))
+
+        offs_sb = keep.tile([P, E * C // 16], U16, name="offs_sb")
+        pos1_sb = keep.tile([P, T // 16], U16, name="pos1_sb")
+        pos2_sb = keep.tile([P, T // 16], U16, name="pos2_sb")
+
+        def cast(engine, dst, src):
+            if engine == "scalar":
+                nc.scalar.copy(out=dst, in_=src)
+            else:
+                nc.vector.tensor_copy(out=dst, in_=src)
+
+        def quantize(pool, vals, words, tag):
+            c = pool.tile([P, words], U32, name="c_" + tag, align_bytes=64)
+            s = pool.tile([P, words], U8, name="s_" + tag, align_bytes=64)
+            nc.vector.quantize_mx(out=c[:].bitcast(FP8X4), scales=s[:], in_=vals)
+            return c, s
+
+        warm = keep.tile([P, 2], F32, name="warm")
+        nc.vector.memset(warm[:, 0:1], 0.0)
+        nc.scalar.activation(out=warm[:, 1:2], in_=warm[:, 0:1], func=SILU)
+
+        w1_raw, w2_raw, w1_val, w2_val, w1_codes, w2_codes = {}, {}, {}, {}, {}, {}
+        x_raw, x_val, x_codes, h_val, h_codes, accs = {}, {}, {}, {}, {}, {}
+
+        def load_x(r):
+            t = keep.tile([P, J, C], F32, name="xr%d" % r)
+            nc.sync.dma_start(out=t[:], in_=xT[:, r * C : (r + 1) * C].rearrange("(p j) t -> p j t", j=J))
+            x_raw[r] = t
+
+        def load_w1(e, g):
+            t = raws.tile([P, J, K_PASS], F32, name="w1r")
+            rows = w1[e, :, g * K_PASS : (g + 1) * K_PASS].rearrange("(p j) c -> p j c", j=J)
+            for j in range(0, J, J_PIECE):
+                nc.sync.dma_start(out=t[:, j : j + J_PIECE, :], in_=rows[:, j : j + J_PIECE, :])
+            w1_raw[e, g] = t
+
+        def load_w2(e):
+            t = raws2.tile([P, HALVES, J, N], F32, name="w2r")
+            nc.sync.dma_start(
+                out=t[:].rearrange("p g j n -> p g (j n)"),
+                in_=w2[e].rearrange("(g p j) n -> p g (j n)", g=HALVES, j=J),
+            )
+            w2_raw[e] = t
+
+        y_sb = keep.tile([P, E * C], F32, name="y_sb")
+        gate_sb = keep.tile([P, 2, T], F32, name="gate_sb")
+
+        pairs = []
+        for u in range(2):
+            pt = keep.tile([P, T, 2], BF16, name="pair%d" % u)
+            pairs.append(pt)
+
+        def cast_pairs(r):
+            for u in range(2):
+                cast(
+                    "vector",
+                    pairs[u][:, r * C : (r + 1) * C, :].rearrange("p (c i) e -> p c e i", i=4),
+                    x_raw[r][:, 2 * u : 2 * u + 2, :].rearrange("p e (c i) -> p c e i", i=4),
+                )
+
+        def cast_x(r):
+            t = values.tile([P, C, J], BF16, name="xv", align_bytes=64)
+            cast(
+                "scalar",
+                t[:].rearrange("p (c i) j -> p c j i", i=4),
+                x_raw[r][:].rearrange("p j (c i) -> p c j i", i=4),
+            )
+            x_val[E + r] = t
+
+        def gather_x(e, u):
+            if u == 0:
+                t = single.tile([P, C, J], BF16, name="xg", align_bytes=64)
+                x_val[e] = t
+            words = x_val[e][:].rearrange("p n j -> p (n j)").bitcast(U32).rearrange("p (n u) -> p n u", u=2)
+            window = pairs[u][:].rearrange("p t e -> p (t e)").bitcast(U32)
+            nc.vector.tensor_copy(out=words[:, :, u], in_=window.indirect(offs_sb[:, e * C // 16 : (e + 1) * C // 16]))
+
+        def quantize_x(q):
+            x_codes[q] = quantize(keep if q >= E else pair, x_val[q][:].rearrange("p n j -> p (n j)"), C, "x%d" % q if q >= E else "x")
+
+        def cast_w1(e, g):
+            t = single.tile([P, J, P, J], BF16, name="w1v%d" % g, align_bytes=64)
+            cast(
+                "scalar" if (e, g) in SCALAR_W1 else "vector",
+                t[:].rearrange("p t m j -> p m j t"),
+                w1_raw[e, g][:].rearrange("p j (m t) -> p m j t", t=J),
+            )
+            w1_val[e, g] = t
+
+        def quantize_w1(e, g):
+            w1_codes[e, g] = quantize(codes, w1_val[e, g][:].rearrange("p t m j -> p (t m j)"), K_PASS, "w1")
+
+        def cast_w2(e):
+            t = single.tile([P, HALVES, N, J], BF16, name="w2v", align_bytes=64)
+            for g in range(HALVES):
+                cast(
+                    "scalar" if e in SCALAR_W2 else "vector",
+                    t[:, g].rearrange("p (c i) j -> p c j i", i=4),
+                    w2_raw[e][:, g].rearrange("p j (c i) -> p c j i", i=4),
+                )
+            w2_val[e] = t
+
+        def quantize_w2(e):
+            w2_codes[e] = quantize(codes, w2_val[e][:].rearrange("p g n j -> p (g n j)"), HALVES * N, "w2")
+
+        def first_layer(e, q, g):
+            wc, ws = w1_codes[e, g]
+            xc, xs = x_codes[q]
+            hv = hidden.tile([P, C, J], BF16, name="hv", align_bytes=64)
+            for s in range(C // P):
+                bank = psum_a.tile([P, J, P], F32, name="bank")
+                cols = slice(s * P, (s + 1) * P)
+                for t in range(J):
+                    rows = slice(t * P, (t + 1) * P)
+                    nc.tensor.matmul_mx(
+                        out=bank[:, t, :],
+                        lhsT=wc[:, rows].bitcast(FP8X4),
+                        lhsT_scale=ws[:, rows],
+                        rhs=xc[:, cols].bitcast(FP8X4),
+                        rhs_scale=xs[:, cols],
+                        start=True,
+                        stop=True,
+                    )
+                nc.scalar.activation(out=hv[:, cols, :], in_=bank[:].rearrange("p t n -> p n t"), func=SILU)
+            h_val[q, g] = hv
+
+        def quantize_h(q, g):
+            h_codes[q, g] = quantize(hidden, h_val[q, g][:].rearrange("p n j -> p (n j)"), C, "h")
+
+        def second_layer(e, q, g):
+            wc, ws = w2_codes[e]
+            hc, hs = h_codes[q, g]
+            if g == 1:
+                acc = psum_y.tile([P, C], F32, name="acc")
+                accs[q] = acc
+            rows = slice(g * N, (g + 1) * N)
+            nc.tensor.matmul_mx(
+                out=accs[q][:],
+                lhsT=wc[:, rows].bitcast(FP8X4),
+                lhsT_scale=ws[:, rows],
+                rhs=hc[:].bitcast(FP8X4),
+                rhs_scale=hs[:],
+                start=(g == 1),
+                stop=(g == 0),
+            )
+
+        def keep_y(e):
+            nc.vector.tensor_copy(out=y_sb[:, e * C : (e + 1) * C], in_=accs[e][:])
+
+        picked = {}
+
+        def pick(r, pos):
+            t = keep.tile([P, T], F32, name="picked%d" % r)
+            nc.vector.tensor_tensor(out=t[:], in0=y_sb[:].indirect(pos[:]), in1=gate_sb[:, r, :], op=MULT)
+            picked[r] = t
+
+        def load_gate():
+            for r in range(2):
+                nc.sync.dma_start(out=gate_sb[:, r, :], in_=gate[r])
+
+        def load_expert(e):
+            if e <= E:
+                load_w1(e, 1)
+                load_w1(e, 0)
+                if e > 0:
+                    load_w2(e - 1)
+            if e == E:
+                load_gate()
+                load_w2(E)
+
+        for r in range(SHARED_GROUPS):
+            load_x(r)
+        nc.sync.dma_start(offs_sb[:], offs)
+        load_expert(0)
+        load_expert(1)
+        nc.sync.dma_start(pos1_sb[:], pos1)
+        nc.sync.dma_start(pos2_sb[:], pos2)
+        load_expert(2)
+        for r in range(SHARED_GROUPS):
+            cast_pairs(r)
+            cast_x(r)
+        cast_w1(0, 1)
+        gather_x(0, 0)
+        gather_x(0, 1)
+        quantize_x(E)
+        quantize_x(0)
+        quantize_x(E + 1)
+        quantize_x(E + 2)
+
+        for e in range(E):
+            load_expert(e + 3)
+            cast_w1(e, 0)
+            if e > 0:
+                cast_w1(e, 1)
+            else:
+                quantize_w1(e, 1)
+                first_layer(e, e, 1)
+            if e > 0:
+                cast_w2(e - 1)
+                quantize_h(e - 1, 1)
+            if e + 1 < E:
+                gather_x(e + 1, 0)
+            if e > 0:
+                quantize_w1(e, 1)
+                first_layer(e, e, 1)
+            if e + 1 < E:
+                gather_x(e + 1, 1)
+            quantize_w1(e, 0)
+            first_layer(e, e, 0)
+            if e > 1:
+                keep_y(e - 2)
+            if e > 0:
+                quantize_h(e - 1, 0)
+            if e + 1 < E:
+                quantize_x(e + 1)
+            if e > 0:
+                quantize_w2(e - 1)
+                second_layer(e - 1, e - 1, 1)
+                second_layer(e - 1, e - 1, 0)
+
+        routed = keep.tile([P, T], F32, name="routed")
+
+        def finish(r):
+            second_layer(SHARED, E + r, 1)
+            second_layer(SHARED, E + r, 0)
+            cols = slice(r * C, (r + 1) * C)
+            res = keep.tile([P, C], F32, name="res%d" % r)
+            nc.vector.tensor_tensor(out=res[:], in0=routed[:, cols], in1=accs[E + r][:], op=ADD)
+            nc.sync.dma_start(out=out[:, cols], in_=res[:])
+
+        cast_w1(SHARED, 0)
+        cast_w1(SHARED, 1)
+        cast_w2(E - 1)
+        quantize_h(E - 1, 1)
+        quantize_w1(SHARED, 1)
+        first_layer(SHARED, E, 1)
+        first_layer(SHARED, E + 1, 1)
+        quantize_h(E - 1, 0)
+        keep_y(E - 2)
+        quantize_w1(SHARED, 0)
+        quantize_w2(E - 1)
+        second_layer(E - 1, E - 1, 1)
+        second_layer(E - 1, E - 1, 0)
+        first_layer(SHARED, E + 2, 1)
+        quantize_h(E, 1)
+        keep_y(E - 1)
+        cast_w2(SHARED)
+        first_layer(SHARED, E, 0)
+        pick(0, pos1_sb)
+        quantize_h(E + 1, 1)
+        first_layer(SHARED, E + 1, 0)
+        pick(1, pos2_sb)
+        quantize_h(E + 2, 1)
+        first_layer(SHARED, E + 2, 0)
+        quantize_w2(SHARED)
+        quantize_h(E, 0)
+        nc.vector.tensor_tensor(out=routed[:], in0=picked[0][:], in1=picked[1][:], op=ADD)
+        quantize_h(E + 1, 0)
+        finish(0)
+        quantize_h(E + 2, 0)
+        finish(1)
+        finish(2)

@@ -21,31 +21,41 @@ K_PASS = P * J
 HALVES = H // K_PASS
 SHARED = E
 SHARED_GROUPS = T // C
-SCALAR_W1 = [(0, 1)] + [(e, 0) for e in range(E + 1)]
-SCALAR_W2 = [0, 1, 2, 3, 6]
-J_PIECE = 2
+PC = 2 * C
+SCALAR_W1 = [(0, 1), (0, 0), (1, 0), (2, 0), (3, 0), (4, 0), (5, 0), (6, 0)]
+W2_ENGINE = "SVVSVVS"
+SCALAR_Y = []
+J_PIECE = [2, 2, 2, 2, 2, 2, 2]
+RINGS = dict(w1r=5, w1s=5, w2r=5, xv=3, xg=2, xp=1, x=4, w1v=2, w2v=2, w1=4, w2=3, hv=3, h=7, bank=4, acc=3)
+FORCED = 6
+AHEAD = 3
+GATHER_PLAIN = False
+OFFS_AFTER = 2
+W2_AFTER = 1
+SEQ = [("C0", -1), ("G0", -2), ("C1", -1), ("M1", 0), ("G1", -2), ("Q0", -1), ("Q1", -1), ("M0", 0), ("CW", 0), ("Y", 3), ("H0", 0), ("QX", -2), ("QW", 0), ("Y", 2), ("S", 0)]
+HEAD = ["X0", "X1", "X2", "C10", "C00", "G00", "G10", "QX6", "QX0", "QX7", "QX8", "Q10", "G01", "G11", "Q00", "QX1"]
+TAIL = ["C06", "C16", "Q16", "Q06", "CW6", "M16.0", "M16.1", "Y1", "M16.2", "Y2", "P0", "H16.0", "M06.0", "H16.1", "M06.1", "P1", "H16.2", "M06.2", "H06.0", "QW6", "ADD", "H06.1", "H06.2", "F0", "F1", "F2"]
 
 
 def tile_moe_shr_mlp_silu_kernel(tc, xT, w1, w2, gate, offs, pos1, pos2, out):
     nc = tc.nc
     with ExitStack() as ctx:
         keep = ctx.enter_context(tc.tile_pool(name="keep", bufs=1))
-        raws = ctx.enter_context(tc.tile_pool(name="raws", bufs=8))
-        raws2 = ctx.enter_context(tc.tile_pool(name="raws2", bufs=7))
-        values = ctx.enter_context(tc.tile_pool(name="values", bufs=4))
-        single = ctx.enter_context(tc.tile_pool(name="single", bufs=2))
-        pair = ctx.enter_context(tc.tile_pool(name="pair", bufs=2))
-        codes = ctx.enter_context(tc.tile_pool(name="codes", bufs=4))
-        hidden = ctx.enter_context(tc.tile_pool(name="hidden", bufs=10))
-        psum_a = ctx.enter_context(tc.psum_pool(name="psum_a", bufs=5))
-        psum_y = ctx.enter_context(tc.psum_pool(name="psum_y", bufs=3))
+        rings = {}
+        for tag in RINGS:
+            if tag not in ("bank", "acc"):
+                rings[tag] = ctx.enter_context(tc.tile_pool(name=tag, bufs=RINGS[tag]))
+        psum_a = ctx.enter_context(tc.psum_pool(name="psum_a", bufs=RINGS["bank"]))
+        psum_y = ctx.enter_context(tc.psum_pool(name="psum_y", bufs=RINGS["acc"]))
 
         offs_sb = keep.tile([P, E * C // 16], U16, name="offs_sb")
         pos1_sb = keep.tile([P, T // 16], U16, name="pos1_sb")
         pos2_sb = keep.tile([P, T // 16], U16, name="pos2_sb")
 
         def cast(engine, dst, src):
-            if engine == "scalar":
+            if engine == "P":
+                nc.gpsimd.tensor_scalar(out=dst, in0=src, scalar1=1.0, scalar2=0.0, op0=MULT, op1=ADD)
+            elif engine in ("scalar", "S"):
                 nc.scalar.copy(out=dst, in_=src)
             else:
                 nc.vector.tensor_copy(out=dst, in_=src)
@@ -69,14 +79,15 @@ def tile_moe_shr_mlp_silu_kernel(tc, xT, w1, w2, gate, offs, pos1, pos2, out):
             x_raw[r] = t
 
         def load_w1(e, g):
-            t = raws.tile([P, J, K_PASS], F32, name="w1r")
+            tag = "w1s" if (e, g) in SCALAR_W1 and e > 0 else "w1r"
+            t = rings[tag].tile([P, J, K_PASS], F32, name=tag, align_bytes=64)
             rows = w1[e, :, g * K_PASS : (g + 1) * K_PASS].rearrange("(p j) c -> p j c", j=J)
-            for j in range(0, J, J_PIECE):
-                nc.sync.dma_start(out=t[:, j : j + J_PIECE, :], in_=rows[:, j : j + J_PIECE, :])
+            for j in range(0, J, J_PIECE[e]):
+                nc.sync.dma_start(out=t[:, j : j + J_PIECE[e], :], in_=rows[:, j : j + J_PIECE[e], :])
             w1_raw[e, g] = t
 
         def load_w2(e):
-            t = raws2.tile([P, HALVES, J, N], F32, name="w2r")
+            t = rings["w2r"].tile([P, HALVES, J, N], F32, name="w2r")
             nc.sync.dma_start(
                 out=t[:].rearrange("p g j n -> p g (j n)"),
                 in_=w2[e].rearrange("(g p j) n -> p g (j n)", g=HALVES, j=J),
@@ -100,7 +111,7 @@ def tile_moe_shr_mlp_silu_kernel(tc, xT, w1, w2, gate, offs, pos1, pos2, out):
                 )
 
         def cast_x(r):
-            t = values.tile([P, C, J], BF16, name="xv", align_bytes=64)
+            t = rings["xv"].tile([P, C, J], BF16, name="xv", align_bytes=64)
             cast(
                 "scalar",
                 t[:].rearrange("p (c i) j -> p c j i", i=4),
@@ -109,18 +120,36 @@ def tile_moe_shr_mlp_silu_kernel(tc, xT, w1, w2, gate, offs, pos1, pos2, out):
             x_val[E + r] = t
 
         def gather_x(e, u):
-            if u == 0:
-                t = single.tile([P, C, J], BF16, name="xg", align_bytes=64)
-                x_val[e] = t
-            words = x_val[e][:].rearrange("p n j -> p (n j)").bitcast(U32).rearrange("p (n u) -> p n u", u=2)
             window = pairs[u][:].rearrange("p t e -> p (t e)").bitcast(U32)
-            nc.vector.tensor_copy(out=words[:, :, u], in_=window.indirect(offs_sb[:, e * C // 16 : (e + 1) * C // 16]))
+            picks = window.indirect(offs_sb[:, e * C // 16 : (e + 1) * C // 16])
+            if GATHER_PLAIN:
+                if u == 0:
+                    xp[e] = rings["xp"].tile([P, 2, C, 2], BF16, name="xp", align_bytes=64)
+                nc.vector.tensor_copy(out=xp[e][:, u].rearrange("p n e -> p (n e)").bitcast(U32), in_=picks)
+            else:
+                if u == 0:
+                    t = rings["xg"].tile([P, C, J], BF16, name="xg", align_bytes=64)
+                    x_val[e] = t
+                words = x_val[e][:].rearrange("p n j -> p (n j)").bitcast(U32).rearrange("p (n u) -> p n u", u=2)
+                nc.vector.tensor_copy(out=words[:, :, u], in_=picks)
+
+        def weave_x(e):
+            if GATHER_PLAIN:
+                t = rings["xg"].tile([P, C, J], BF16, name="xg", align_bytes=64)
+                x_val[e] = t
+                nc.vector.tensor_copy(
+                    out=t[:].rearrange("p n (u e) -> p n u e", u=2), in_=xp[e][:].rearrange("p u n e -> p n u e")
+                )
+
+        xp = {}
 
         def quantize_x(q):
-            x_codes[q] = quantize(keep if q >= E else pair, x_val[q][:].rearrange("p n j -> p (n j)"), C, "x%d" % q if q >= E else "x")
+            pool, tag = (keep, "x%d" % q) if q >= E else (rings["x"], "x")
+            c, s = quantize(pool, x_val[q][:].rearrange("p n j -> p (n j)"), C, tag)
+            x_codes[q] = c[:], s[:]
 
         def cast_w1(e, g):
-            t = single.tile([P, J, P, J], BF16, name="w1v%d" % g, align_bytes=64)
+            t = rings["w1v"].tile([P, J, P, J], BF16, name="w1v%d" % g, align_bytes=64)
             cast(
                 "scalar" if (e, g) in SCALAR_W1 else "vector",
                 t[:].rearrange("p t m j -> p m j t"),
@@ -129,25 +158,24 @@ def tile_moe_shr_mlp_silu_kernel(tc, xT, w1, w2, gate, offs, pos1, pos2, out):
             w1_val[e, g] = t
 
         def quantize_w1(e, g):
-            w1_codes[e, g] = quantize(codes, w1_val[e, g][:].rearrange("p t m j -> p (t m j)"), K_PASS, "w1")
+            w1_codes[e, g] = quantize(rings["w1"], w1_val[e, g][:].rearrange("p t m j -> p (t m j)"), K_PASS, "w1")
 
         def cast_w2(e):
-            t = single.tile([P, HALVES, N, J], BF16, name="w2v", align_bytes=64)
-            for g in range(HALVES):
-                cast(
-                    "scalar" if e in SCALAR_W2 else "vector",
-                    t[:, g].rearrange("p (c i) j -> p c j i", i=4),
-                    w2_raw[e][:, g].rearrange("p j (c i) -> p c j i", i=4),
-                )
+            t = rings["w2v"].tile([P, HALVES, N, J], BF16, name="w2v", align_bytes=64)
+            cast(W2_ENGINE[e], t[:], w2_raw[e][:].rearrange("p g j n -> p g n j"))
             w2_val[e] = t
 
         def quantize_w2(e):
-            w2_codes[e] = quantize(codes, w2_val[e][:].rearrange("p g n j -> p (g n j)"), HALVES * N, "w2")
+            w2_codes[e] = quantize(rings["w2"], w2_val[e][:].rearrange("p g n j -> p (g n j)"), HALVES * N, "w2")
 
         def first_layer(e, q, g):
             wc, ws = w1_codes[e, g]
             xc, xs = x_codes[q]
-            hv = hidden.tile([P, C, J], BF16, name="hv", align_bytes=64)
+            made.add((q, g))
+            if q not in h_val:
+                tag = "w1s" if q < FORCED else "hv"
+                hv = rings[tag].tile([P, HALVES, C, J], BF16, name=tag, align_bytes=64)
+                h_val[q] = hv
             for s in range(C // P):
                 bank = psum_a.tile([P, J, P], F32, name="bank")
                 cols = slice(s * P, (s + 1) * P)
@@ -162,35 +190,58 @@ def tile_moe_shr_mlp_silu_kernel(tc, xT, w1, w2, gate, offs, pos1, pos2, out):
                         start=True,
                         stop=True,
                     )
-                nc.scalar.activation(out=hv[:, cols, :], in_=bank[:].rearrange("p t n -> p n t"), func=SILU)
-            h_val[q, g] = hv
+                nc.scalar.activation(out=h_val[q][:, g, cols, :], in_=bank[:].rearrange("p t n -> p n t"), func=SILU)
+
+        made = set()
 
         def quantize_h(q, g):
-            h_codes[q, g] = quantize(hidden, h_val[q, g][:].rearrange("p n j -> p (n j)"), C, "h")
+            assert (q, g) in made and (q >= E or (q, 1 - g) in made)
+            if q < E:
+                c, s = quantize(rings["h"], h_val[q][:].rearrange("p g n j -> p (g n j)"), HALVES * C, "h")
+                for k in range(HALVES):
+                    h_codes[q, k] = c[:, k * C : (k + 1) * C], s[:, k * C : (k + 1) * C]
+            else:
+                c, s = quantize(rings["h"], h_val[q][:, g].rearrange("p n j -> p (n j)"), C, "h")
+                h_codes[q, g] = c[:], s[:]
 
         def second_layer(e, q, g):
             wc, ws = w2_codes[e]
             hc, hs = h_codes[q, g]
-            if g == 1:
-                acc = psum_y.tile([P, C], F32, name="acc")
-                accs[q] = acc
+            made.add(("y", q))
+            if q < E:
+                if q % 2 == 0 and g == 1:
+                    acc = psum_y.tile([P, 2, C], F32, name="acc")
+                    accs[q] = acc
+                dst = accs[q - q % 2][:, q % 2, :]
+            else:
+                if g == 1:
+                    acc = psum_y.tile([P, C], F32, name="acc")
+                    accs[q] = acc
+                dst = accs[q][:]
             rows = slice(g * N, (g + 1) * N)
             nc.tensor.matmul_mx(
-                out=accs[q][:],
+                out=dst,
                 lhsT=wc[:, rows].bitcast(FP8X4),
                 lhsT_scale=ws[:, rows],
-                rhs=hc[:].bitcast(FP8X4),
-                rhs_scale=hs[:],
+                rhs=hc.bitcast(FP8X4),
+                rhs_scale=hs,
                 start=(g == 1),
                 stop=(g == 0),
             )
 
         def keep_y(e):
-            nc.vector.tensor_copy(out=y_sb[:, e * C : (e + 1) * C], in_=accs[e][:])
+            assert ("y", 2 * e) in made and ("y", 2 * e + 1) in made
+            made.add(("kept", e))
+            cast(
+                "scalar" if e in SCALAR_Y else "vector",
+                y_sb[:, e * PC : (e + 1) * PC],
+                accs[2 * e][:].rearrange("p k n -> p (k n)"),
+            )
 
         picked = {}
 
         def pick(r, pos):
+            assert all(("kept", i) in made for i in range(E // 2))
             t = keep.tile([P, T], F32, name="picked%d" % r)
             nc.vector.tensor_tensor(out=t[:], in0=y_sb[:].indirect(pos[:]), in1=gate_sb[:, r, :], op=MULT)
             picked[r] = t
@@ -199,105 +250,108 @@ def tile_moe_shr_mlp_silu_kernel(tc, xT, w1, w2, gate, offs, pos1, pos2, out):
             for r in range(2):
                 nc.sync.dma_start(out=gate_sb[:, r, :], in_=gate[r])
 
-        def load_expert(e):
-            if e <= E:
-                load_w1(e, 1)
-                load_w1(e, 0)
-                if e > 0:
-                    load_w2(e - 1)
+        loads = []
+        for e in range(E + 1):
+            loads += [("w1", e, 1), ("w1", e, 0)]
+            if e == 1:
+                loads.append(("pos", 0, 0))
+            if e >= W2_AFTER:
+                loads.append(("w2", e - W2_AFTER, 0))
+        for e in range(E + 1 - W2_AFTER, E + 1):
             if e == E:
-                load_gate()
-                load_w2(E)
+                loads.append(("gate", 0, 0))
+            loads.append(("w2", e, 0))
+
+        def load_until(limit):
+            while loads and not (loads[0][0] == "w1" and loads[0][1] > limit):
+                kind, e, g = loads[0]
+                loads.remove(loads[0])
+                if kind == "w1":
+                    load_w1(e, g)
+                elif kind == "w2":
+                    load_w2(e)
+                elif kind == "pos":
+                    nc.sync.dma_start(pos1_sb[:], pos1)
+                    nc.sync.dma_start(pos2_sb[:], pos2)
+                else:
+                    load_gate()
+
+        routed = keep.tile([P, T], F32, name="routed")
+        done = set()
+
+        def run(op, e, r=None):
+            key = (op, e, r)
+            if key in done:
+                return
+            done.add(key)
+            if op == "X":
+                cast_pairs(e)
+                cast_x(e)
+            elif op in ("C0", "C1"):
+                cast_w1(e, int(op[1]))
+            elif op == "CW":
+                cast_w2(e)
+            elif op in ("G0", "G1"):
+                gather_x(e, int(op[1]))
+            elif op == "W":
+                weave_x(e)
+            elif op == "QX":
+                quantize_x(e)
+            elif op in ("Q0", "Q1"):
+                quantize_w1(e, int(op[1]))
+            elif op in ("M0", "M1"):
+                first_layer(e, e + (r or 0), int(op[1]))
+            elif op in ("H0", "H1"):
+                quantize_h(e + (r or 0), int(op[1]))
+            elif op == "QW":
+                quantize_w2(e)
+            elif op == "S":
+                second_layer(e, e, 1)
+                second_layer(e, e, 0)
+            elif op == "Y":
+                keep_y(e)
+            elif op == "P":
+                pick(e, (pos1_sb, pos2_sb)[e])
+            elif op == "A":
+                nc.vector.tensor_tensor(out=routed[:], in0=picked[0][:], in1=picked[1][:], op=ADD)
+            elif op == "F":
+                second_layer(SHARED, E + e, 1)
+                second_layer(SHARED, E + e, 0)
+                cols = slice(e * C, (e + 1) * C)
+                res = keep.tile([P, C], F32, name="res%d" % e)
+                nc.vector.tensor_tensor(out=res[:], in0=routed[:, cols], in1=accs[E + e][:], op=ADD)
+                nc.sync.dma_start(out=out[:, cols], in_=res[:])
+
+        def text(s):
+            if s[:2] == "QP":
+                return ("QP", int(s[2:]), None)
+            if s == "ADD":
+                return ("A", 0, None)
+            r = None
+            if "." in s:
+                s, r = s.split(".")
+                r = int(r)
+            if s[0] in "XPFSYW":
+                return (s[0], int(s[1:]), r)
+            return (s[:2], int(s[2:]), r)
 
         for r in range(SHARED_GROUPS):
             load_x(r)
-        nc.sync.dma_start(offs_sb[:], offs)
-        load_expert(0)
-        load_expert(1)
-        nc.sync.dma_start(pos1_sb[:], pos1)
-        nc.sync.dma_start(pos2_sb[:], pos2)
-        load_expert(2)
-        for r in range(SHARED_GROUPS):
-            cast_pairs(r)
-            cast_x(r)
-        cast_w1(0, 1)
-        gather_x(0, 0)
-        gather_x(0, 1)
-        quantize_x(E)
-        quantize_x(0)
-        quantize_x(E + 1)
-        quantize_x(E + 2)
-
-        for e in range(E):
-            load_expert(e + 3)
-            cast_w1(e, 0)
-            if e > 0:
-                cast_w1(e, 1)
-            else:
-                quantize_w1(e, 1)
-                first_layer(e, e, 1)
-            if e > 0:
-                cast_w2(e - 1)
-                quantize_h(e - 1, 1)
-            if e + 1 < E:
-                gather_x(e + 1, 0)
-            if e > 0:
-                quantize_w1(e, 1)
-                first_layer(e, e, 1)
-            if e + 1 < E:
-                gather_x(e + 1, 1)
-            quantize_w1(e, 0)
-            first_layer(e, e, 0)
-            if e > 1:
-                keep_y(e - 2)
-            if e > 0:
-                quantize_h(e - 1, 0)
-            if e + 1 < E:
-                quantize_x(e + 1)
-            if e > 0:
-                quantize_w2(e - 1)
-                second_layer(e - 1, e - 1, 1)
-                second_layer(e - 1, e - 1, 0)
-
-        routed = keep.tile([P, T], F32, name="routed")
-
-        def finish(r):
-            second_layer(SHARED, E + r, 1)
-            second_layer(SHARED, E + r, 0)
-            cols = slice(r * C, (r + 1) * C)
-            res = keep.tile([P, C], F32, name="res%d" % r)
-            nc.vector.tensor_tensor(out=res[:], in0=routed[:, cols], in1=accs[E + r][:], op=ADD)
-            nc.sync.dma_start(out=out[:, cols], in_=res[:])
-
-        cast_w1(SHARED, 0)
-        cast_w1(SHARED, 1)
-        cast_w2(E - 1)
-        quantize_h(E - 1, 1)
-        quantize_w1(SHARED, 1)
-        first_layer(SHARED, E, 1)
-        first_layer(SHARED, E + 1, 1)
-        quantize_h(E - 1, 0)
-        keep_y(E - 2)
-        quantize_w1(SHARED, 0)
-        quantize_w2(E - 1)
-        second_layer(E - 1, E - 1, 1)
-        second_layer(E - 1, E - 1, 0)
-        first_layer(SHARED, E + 2, 1)
-        quantize_h(E, 1)
-        keep_y(E - 1)
-        cast_w2(SHARED)
-        first_layer(SHARED, E, 0)
-        pick(0, pos1_sb)
-        quantize_h(E + 1, 1)
-        first_layer(SHARED, E + 1, 0)
-        pick(1, pos2_sb)
-        quantize_h(E + 2, 1)
-        first_layer(SHARED, E + 2, 0)
-        quantize_w2(SHARED)
-        quantize_h(E, 0)
-        nc.vector.tensor_tensor(out=routed[:], in0=picked[0][:], in1=picked[1][:], op=ADD)
-        quantize_h(E + 1, 0)
-        finish(0)
-        quantize_h(E + 2, 0)
-        finish(1)
-        finish(2)
+            if r == OFFS_AFTER:
+                nc.sync.dma_start(offs_sb[:], offs)
+        load_until(AHEAD - 1)
+        for s in HEAD:
+            if len(s) == 2 and s[0] != "X":
+                s = s + "0"
+            run(*text(s))
+        for i in range(E):
+            load_until(i + AHEAD)
+            for op, lag in SEQ:
+                e = i - lag
+                if op == "Y":
+                    if e % 2 == 0 and 0 <= e // 2 < E // 2:
+                        run(op, e // 2)
+                elif 0 <= e < E or (e == E and op in ("C0", "C1", "Q0", "Q1")):
+                    run(op, e)
+        for s in TAIL:
+            run(*text(s))

from contextlib import ExitStack

import concourse.mybir as mybir

K, T, E, C, H, N = 512, 768, 6, 256, 1024, 128
FLOPS = 2 * (E * C + T) * (K * H + H * N)

F32 = mybir.dt.float32
BF16 = mybir.dt.bfloat16
U32 = mybir.dt.uint32
U16 = mybir.dt.uint16
U8 = mybir.dt.uint8
FP8X4 = mybir.dt.float8_e4m3fn_x4
SILU = mybir.ActivationFunctionType.Silu
ADD = mybir.AluOpType.add
MULT = mybir.AluOpType.mult

P = 128
J = 4
K_PASS = P * J
HALVES = H // K_PASS
SHARED = E
SHARED_GROUPS = T // C
PC = 2 * C
SCALAR_W1 = [(0, 1), (0, 0), (1, 0), (2, 0), (3, 0), (4, 0), (5, 0), (6, 0)]
W2_ENGINE = "SVVSVVS"
SCALAR_Y = []
J_PIECE = [2, 2, 2, 2, 2, 2, 2]
RINGS = dict(w1r=5, w1s=5, w2r=5, xv=3, xg=2, xp=1, x=4, w1v=2, w2v=2, w1=4, w2=3, hv=3, h=7, bank=4, acc=3)
FORCED = 6
AHEAD = 3
GATHER_PLAIN = False
OFFS_AFTER = 2
W2_AFTER = 1
SEQ = [("C0", -1), ("G0", -2), ("C1", -1), ("M1", 0), ("G1", -2), ("Q0", -1), ("Q1", -1), ("M0", 0), ("CW", 0), ("Y", 3), ("H0", 0), ("QX", -2), ("QW", 0), ("Y", 2), ("S", 0)]
HEAD = ["X0", "X1", "X2", "C10", "C00", "G00", "G10", "QX6", "QX0", "QX7", "QX8", "Q10", "G01", "G11", "Q00", "QX1"]
TAIL = ["C06", "C16", "Q16", "Q06", "CW6", "M16.0", "M16.1", "Y1", "M16.2", "Y2", "P0", "H16.0", "M06.0", "H16.1", "M06.1", "P1", "H16.2", "M06.2", "H06.0", "QW6", "ADD", "H06.1", "H06.2", "F0", "F1", "F2"]


def tile_moe_shr_mlp_silu_kernel(tc, xT, w1, w2, gate, offs, pos1, pos2, out):
    nc = tc.nc
    with ExitStack() as ctx:
        keep = ctx.enter_context(tc.tile_pool(name="keep", bufs=1))
        rings = {}
        for tag in RINGS:
            if tag not in ("bank", "acc"):
                rings[tag] = ctx.enter_context(tc.tile_pool(name=tag, bufs=RINGS[tag]))
        psum_a = ctx.enter_context(tc.psum_pool(name="psum_a", bufs=RINGS["bank"]))
        psum_y = ctx.enter_context(tc.psum_pool(name="psum_y", bufs=RINGS["acc"]))

        offs_sb = keep.tile([P, E * C // 16], U16, name="offs_sb")
        pos1_sb = keep.tile([P, T // 16], U16, name="pos1_sb")
        pos2_sb = keep.tile([P, T // 16], U16, name="pos2_sb")

        def cast(engine, dst, src):
            if engine == "P":
                nc.gpsimd.tensor_scalar(out=dst, in0=src, scalar1=1.0, scalar2=0.0, op0=MULT, op1=ADD)
            elif engine in ("scalar", "S"):
                nc.scalar.copy(out=dst, in_=src)
            else:
                nc.vector.tensor_copy(out=dst, in_=src)

        def quantize(pool, vals, words, tag):
            c = pool.tile([P, words], U32, name="c_" + tag, align_bytes=64)
            s = pool.tile([P, words], U8, name="s_" + tag, align_bytes=64)
            nc.vector.quantize_mx(out=c[:].bitcast(FP8X4), scales=s[:], in_=vals)
            return c, s

        warm = keep.tile([P, 2], F32, name="warm")
        nc.vector.memset(warm[:, 0:1], 0.0)
        nc.scalar.activation(out=warm[:, 1:2], in_=warm[:, 0:1], func=SILU)

        w1_raw, w2_raw, w1_val, w2_val, w1_codes, w2_codes = {}, {}, {}, {}, {}, {}
        x_raw, x_val, x_codes, h_val, h_codes, accs = {}, {}, {}, {}, {}, {}

        def load_x(r):
            t = keep.tile([P, J, C], F32, name="xr%d" % r)
            nc.sync.dma_start(out=t[:], in_=xT[:, r * C : (r + 1) * C].rearrange("(p j) t -> p j t", j=J))
            x_raw[r] = t

        def load_w1(e, g):
            tag = "w1s" if (e, g) in SCALAR_W1 and e > 0 else "w1r"
            t = rings[tag].tile([P, J, K_PASS], F32, name=tag, align_bytes=64)
            rows = w1[e, :, g * K_PASS : (g + 1) * K_PASS].rearrange("(p j) c -> p j c", j=J)
            for j in range(0, J, J_PIECE[e]):
                nc.sync.dma_start(out=t[:, j : j + J_PIECE[e], :], in_=rows[:, j : j + J_PIECE[e], :])
            w1_raw[e, g] = t

        def load_w2(e):
            t = rings["w2r"].tile([P, HALVES, J, N], F32, name="w2r")
            nc.sync.dma_start(
                out=t[:].rearrange("p g j n -> p g (j n)"),
                in_=w2[e].rearrange("(g p j) n -> p g (j n)", g=HALVES, j=J),
            )
            w2_raw[e] = t

        y_sb = keep.tile([P, E * C], F32, name="y_sb")
        gate_sb = keep.tile([P, 2, T], F32, name="gate_sb")

        pairs = []
        for u in range(2):
            pt = keep.tile([P, T, 2], BF16, name="pair%d" % u)
            pairs.append(pt)

        def cast_pairs(r):
            for u in range(2):
                cast(
                    "vector",
                    pairs[u][:, r * C : (r + 1) * C, :].rearrange("p (c i) e -> p c e i", i=4),
                    x_raw[r][:, 2 * u : 2 * u + 2, :].rearrange("p e (c i) -> p c e i", i=4),
                )

        def cast_x(r):
            t = rings["xv"].tile([P, C, J], BF16, name="xv", align_bytes=64)
            cast(
                "scalar",
                t[:].rearrange("p (c i) j -> p c j i", i=4),
                x_raw[r][:].rearrange("p j (c i) -> p c j i", i=4),
            )
            x_val[E + r] = t

        def gather_x(e, u):
            window = pairs[u][:].rearrange("p t e -> p (t e)").bitcast(U32)
            picks = window.indirect(offs_sb[:, e * C // 16 : (e + 1) * C // 16])
            if GATHER_PLAIN:
                if u == 0:
                    xp[e] = rings["xp"].tile([P, 2, C, 2], BF16, name="xp", align_bytes=64)
                nc.vector.tensor_copy(out=xp[e][:, u].rearrange("p n e -> p (n e)").bitcast(U32), in_=picks)
            else:
                if u == 0:
                    t = rings["xg"].tile([P, C, J], BF16, name="xg", align_bytes=64)
                    x_val[e] = t
                words = x_val[e][:].rearrange("p n j -> p (n j)").bitcast(U32).rearrange("p (n u) -> p n u", u=2)
                nc.vector.tensor_copy(out=words[:, :, u], in_=picks)

        def weave_x(e):
            if GATHER_PLAIN:
                t = rings["xg"].tile([P, C, J], BF16, name="xg", align_bytes=64)
                x_val[e] = t
                nc.vector.tensor_copy(
                    out=t[:].rearrange("p n (u e) -> p n u e", u=2), in_=xp[e][:].rearrange("p u n e -> p n u e")
                )

        xp = {}

        def quantize_x(q):
            pool, tag = (keep, "x%d" % q) if q >= E else (rings["x"], "x")
            c, s = quantize(pool, x_val[q][:].rearrange("p n j -> p (n j)"), C, tag)
            x_codes[q] = c[:], s[:]

        def cast_w1(e, g):
            t = rings["w1v"].tile([P, J, P, J], BF16, name="w1v%d" % g, align_bytes=64)
            cast(
                "scalar" if (e, g) in SCALAR_W1 else "vector",
                t[:].rearrange("p t m j -> p m j t"),
                w1_raw[e, g][:].rearrange("p j (m t) -> p m j t", t=J),
            )
            w1_val[e, g] = t

        def quantize_w1(e, g):
            w1_codes[e, g] = quantize(rings["w1"], w1_val[e, g][:].rearrange("p t m j -> p (t m j)"), K_PASS, "w1")

        def cast_w2(e):
            t = rings["w2v"].tile([P, HALVES, N, J], BF16, name="w2v", align_bytes=64)
            cast(W2_ENGINE[e], t[:], w2_raw[e][:].rearrange("p g j n -> p g n j"))
            w2_val[e] = t

        def quantize_w2(e):
            w2_codes[e] = quantize(rings["w2"], w2_val[e][:].rearrange("p g n j -> p (g n j)"), HALVES * N, "w2")

        def first_layer(e, q, g):
            wc, ws = w1_codes[e, g]
            xc, xs = x_codes[q]
            made.add((q, g))
            if q not in h_val:
                tag = "w1s" if q < FORCED else "hv"
                hv = rings[tag].tile([P, HALVES, C, J], BF16, name=tag, align_bytes=64)
                h_val[q] = hv
            for s in range(C // P):
                bank = psum_a.tile([P, J, P], F32, name="bank")
                cols = slice(s * P, (s + 1) * P)
                for t in range(J):
                    rows = slice(t * P, (t + 1) * P)
                    nc.tensor.matmul_mx(
                        out=bank[:, t, :],
                        lhsT=wc[:, rows].bitcast(FP8X4),
                        lhsT_scale=ws[:, rows],
                        rhs=xc[:, cols].bitcast(FP8X4),
                        rhs_scale=xs[:, cols],
                        start=True,
                        stop=True,
                    )
                nc.scalar.activation(out=h_val[q][:, g, cols, :], in_=bank[:].rearrange("p t n -> p n t"), func=SILU)

        made = set()

        def quantize_h(q, g):
            assert (q, g) in made and (q >= E or (q, 1 - g) in made)
            if q < E:
                c, s = quantize(rings["h"], h_val[q][:].rearrange("p g n j -> p (g n j)"), HALVES * C, "h")
                for k in range(HALVES):
                    h_codes[q, k] = c[:, k * C : (k + 1) * C], s[:, k * C : (k + 1) * C]
            else:
                c, s = quantize(rings["h"], h_val[q][:, g].rearrange("p n j -> p (n j)"), C, "h")
                h_codes[q, g] = c[:], s[:]

        def second_layer(e, q, g):
            wc, ws = w2_codes[e]
            hc, hs = h_codes[q, g]
            made.add(("y", q))
            if q < E:
                if q % 2 == 0 and g == 1:
                    acc = psum_y.tile([P, 2, C], F32, name="acc")
                    accs[q] = acc
                dst = accs[q - q % 2][:, q % 2, :]
            else:
                if g == 1:
                    acc = psum_y.tile([P, C], F32, name="acc")
                    accs[q] = acc
                dst = accs[q][:]
            rows = slice(g * N, (g + 1) * N)
            nc.tensor.matmul_mx(
                out=dst,
                lhsT=wc[:, rows].bitcast(FP8X4),
                lhsT_scale=ws[:, rows],
                rhs=hc.bitcast(FP8X4),
                rhs_scale=hs,
                start=(g == 1),
                stop=(g == 0),
            )

        def keep_y(e):
            assert ("y", 2 * e) in made and ("y", 2 * e + 1) in made
            made.add(("kept", e))
            cast(
                "scalar" if e in SCALAR_Y else "vector",
                y_sb[:, e * PC : (e + 1) * PC],
                accs[2 * e][:].rearrange("p k n -> p (k n)"),
            )

        picked = {}

        def pick(r, pos):
            assert all(("kept", i) in made for i in range(E // 2))
            t = keep.tile([P, T], F32, name="picked%d" % r)
            nc.vector.tensor_tensor(out=t[:], in0=y_sb[:].indirect(pos[:]), in1=gate_sb[:, r, :], op=MULT)
            picked[r] = t

        def load_gate():
            for r in range(2):
                nc.sync.dma_start(out=gate_sb[:, r, :], in_=gate[r])

        loads = []
        for e in range(E + 1):
            loads += [("w1", e, 1), ("w1", e, 0)]
            if e == 1:
                loads.append(("pos", 0, 0))
            if e >= W2_AFTER:
                loads.append(("w2", e - W2_AFTER, 0))
        for e in range(E + 1 - W2_AFTER, E + 1):
            if e == E:
                loads.append(("gate", 0, 0))
            loads.append(("w2", e, 0))

        def load_until(limit):
            while loads and not (loads[0][0] == "w1" and loads[0][1] > limit):
                kind, e, g = loads[0]
                loads.remove(loads[0])
                if kind == "w1":
                    load_w1(e, g)
                elif kind == "w2":
                    load_w2(e)
                elif kind == "pos":
                    nc.sync.dma_start(pos1_sb[:], pos1)
                    nc.sync.dma_start(pos2_sb[:], pos2)
                else:
                    load_gate()

        routed = keep.tile([P, T], F32, name="routed")
        done = set()

        def run(op, e, r=None):
            key = (op, e, r)
            if key in done:
                return
            done.add(key)
            if op == "X":
                cast_pairs(e)
                cast_x(e)
            elif op in ("C0", "C1"):
                cast_w1(e, int(op[1]))
            elif op == "CW":
                cast_w2(e)
            elif op in ("G0", "G1"):
                gather_x(e, int(op[1]))
            elif op == "W":
                weave_x(e)
            elif op == "QX":
                quantize_x(e)
            elif op in ("Q0", "Q1"):
                quantize_w1(e, int(op[1]))
            elif op in ("M0", "M1"):
                first_layer(e, e + (r or 0), int(op[1]))
            elif op in ("H0", "H1"):
                quantize_h(e + (r or 0), int(op[1]))
            elif op == "QW":
                quantize_w2(e)
            elif op == "S":
                second_layer(e, e, 1)
                second_layer(e, e, 0)
            elif op == "Y":
                keep_y(e)
            elif op == "P":
                pick(e, (pos1_sb, pos2_sb)[e])
            elif op == "A":
                nc.vector.tensor_tensor(out=routed[:], in0=picked[0][:], in1=picked[1][:], op=ADD)
            elif op == "F":
                second_layer(SHARED, E + e, 1)
                second_layer(SHARED, E + e, 0)
                cols = slice(e * C, (e + 1) * C)
                res = keep.tile([P, C], F32, name="res%d" % e)
                nc.vector.tensor_tensor(out=res[:], in0=routed[:, cols], in1=accs[E + e][:], op=ADD)
                nc.sync.dma_start(out=out[:, cols], in_=res[:])

        def text(s):
            if s[:2] == "QP":
                return ("QP", int(s[2:]), None)
            if s == "ADD":
                return ("A", 0, None)
            r = None
            if "." in s:
                s, r = s.split(".")
                r = int(r)
            if s[0] in "XPFSYW":
                return (s[0], int(s[1:]), r)
            return (s[:2], int(s[2:]), r)

        for r in range(SHARED_GROUPS):
            load_x(r)
            if r == OFFS_AFTER:
                nc.sync.dma_start(offs_sb[:], offs)
        load_until(AHEAD - 1)
        for s in HEAD:
            if len(s) == 2 and s[0] != "X":
                s = s + "0"
            run(*text(s))
        for i in range(E):
            load_until(i + AHEAD)
            for op, lag in SEQ:
                e = i - lag
                if op == "Y":
                    if e % 2 == 0 and 0 <= e // 2 < E // 2:
                        run(op, e // 2)
                elif 0 <= e < E or (e == E and op in ("C0", "C1", "Q0", "Q1")):
                    run(op, e)
        for s in TAIL:
            run(*text(s))
